import numpy as np
import ml_dtypes


def mxq(x, axis, fmt="e4m3"):
    dtype, down = {"e4m3": (ml_dtypes.float8_e4m3fn, 7), "e5m2": (ml_dtypes.float8_e5m2, 14)}[fmt]
    v = np.moveaxis(np.asarray(x, np.float32).astype(ml_dtypes.bfloat16).astype(np.float64), axis, -1)
    blocks = v.reshape(v.shape[:-1] + (-1, 32))
    amax = np.abs(blocks).max(-1, keepdims=True)
    byte = np.maximum(np.where(amax > 0, np.frexp(amax)[1] - 1 + 127, 0) - down, 1)
    scale = np.exp2(byte - 127.0)
    codes = (blocks / scale).astype(np.float32).astype(dtype).astype(np.float64)
    return np.moveaxis((codes * scale).reshape(v.shape), -1, axis)


WIDE = False


def mx_kscale(k):
    if not WIDE:
        return np.ones(k)
    levels = np.array([10, -10, 5, -5, 0])
    if k % 512:
        return np.exp2(np.random.permutation(np.resize(levels, k // 32))).repeat(32)
    a = np.empty((k // 512, 16))
    for p in range(k // 512):
        a[p, :8] = np.random.permutation(np.resize(levels, 8))
        for g in range(8):
            far = levels[np.abs(levels - a[p, g]) >= 10]
            a[p, g + 8] = far[np.random.randint(len(far))]
    return np.exp2(a.ravel()).repeat(32)


BF16 = ml_dtypes.bfloat16


def bf(x):
    return np.asarray(x, np.float32).astype(BF16)


def f64(x):
    return np.asarray(x).astype(np.float64)


E2M1 = np.array([0.0, 0.5, 1.0, 1.5, 2.0, 3.0, 4.0, 6.0, -0.0, -0.5, -1.0, -1.5, -2.0, -3.0, -4.0, -6.0])


def pack_weight(w, fmt):
    k, n = w.shape
    w = f64(bf(w)).reshape(k // 32, 32, n)
    amax = np.abs(w).max(1)
    if fmt == "e4m3":
        byte = np.frexp(amax)[1] - 1 + 127 - 7
    else:
        mant, ex = np.frexp(amax / 6.0)
        byte = np.where(mant > 0.5, ex, ex - 1) + 127
    byte = np.clip(np.where(amax > 0, byte, 1), 1, 254)
    scaled = (w * np.exp2(127.0 - byte)[:, None, :]).reshape(k, n).astype(np.float32)
    by_word = np.ascontiguousarray(scaled.reshape(k // 512, 128, 4, n).transpose(0, 1, 3, 2))
    if fmt == "e4m3":
        words = by_word.astype(ml_dtypes.float8_e4m3fn).view(np.uint8)
    else:
        c = by_word.astype(ml_dtypes.float4_e2m1fn).view(np.uint8) & 0xF
        words = c[..., 0::2] | (c[..., 1::2] << 4)
    return np.ascontiguousarray(words), np.ascontiguousarray(byte.astype(np.uint8).reshape(k // 512, 16, n))


def unpack_weight(words, scales, fmt):
    g, p, n, _ = words.shape
    if fmt == "e4m3":
        vals = np.ascontiguousarray(words).view(ml_dtypes.float8_e4m3fn).astype(np.float64)
    else:
        nib = np.empty((g, p, n, 4), np.uint8)
        nib[..., 0::2] = words & 0xF
        nib[..., 1::2] = words >> 4
        vals = E2M1[nib]
    vals = vals * np.repeat(np.exp2(scales.astype(np.float64) - 127.0), 8, axis=1)[..., None]
    return vals.transpose(0, 1, 3, 2).reshape(g * 512, n)
def pack4(w):
    words, scales = pack_weight(w, "e2m1")
    return words.reshape(words.shape[0], 128, -1), scales


def unpack4(words, scales):
    return unpack_weight(words.reshape(words.shape[0], 128, -1, 2), scales, "e2m1")


M, K, N = 1024, 1024, 1536
STEP = 0.125
ROW_SCALES = (1.0, 1.5, 2.0, 3.0)


def setup_inputs():
    s, t, u = mx_kscale(K), mx_kscale(N), mx_kscale(M)
    alpha = np.random.choice(ROW_SCALES, N) / (2.0 * np.sqrt(K))
    w = np.sign(np.random.standard_normal((K, N))) * alpha
    v_words, v_scales = pack4(w.T / t[:, None])
    return {"x": bf(np.random.standard_normal((M, K)) * s / u[:, None]),
            "wb": bf(w / s[:, None] * t),
            "c": bf((1.0 + 0.25 * np.random.standard_normal((M, N))) / u[:, None] * t),
            "r": bf(STEP * (0.5 + np.random.random(M)) * u * u),
            "v_words": v_words,
            "v_scales": v_scales}


def reference(x, wb, c, r, v_words, v_scales):
    x = f64(x)
    v = unpack4(v_words, v_scales)
    z = mxq(x, 1, "e4m3") @ mxq(f64(wb), 0, "e4m3")
    h = np.maximum(f64(c) - z, 0.0) * f64(r)[:, None]
    dx = mxq(h, 1, "e4m3") @ v
    dw = mxq(x, 0, "e4m3").T @ mxq(h, 0, "e4m3")
    return dx, dw

@@ -1,0 +1,300 @@
+from contextlib import ExitStack
+
+import concourse.mybir as mybir
+from concourse.masks import make_identity
+
+M, K, N = 1024, 1024, 1536
+FLOPS = 3 * 2 * M * K * N
+
+F32 = mybir.dt.float32
+BF16 = mybir.dt.bfloat16
+U32 = mybir.dt.uint32
+I32 = mybir.dt.int32
+U8 = mybir.dt.uint8
+FP8X4 = mybir.dt.float8_e4m3fn_x4
+FP4X4 = mybir.dt.float4_e2m1fn_x4
+ALU = mybir.AluOpType
+
+P = 128
+PACK = 4
+PASS = P * PACK
+G = M // PASS
+A = K // PASS
+J = N // PASS
+UNITS = [(0, 0), (0, 1), (0, 2), (1, 0), (1, 1), (1, 2)]
+AHEAD = 2
+SPLIT = 352
+W12 = 256
+X1_STEP = 7
+X0_ORDER = [(0, 0), (1, 0), (0, 1), (1, 1)]
+X0_STEPS = [6, 10, 12, 14]
+X0_ENG = "ssss"
+X0_LAG = 4
+HT0 = [4, 5, 8, 9, 11, 13]
+HT1 = [23, 23, 24, 24, 25, 26]
+HM = [15, 16, 23, 17, 21, 25]
+HM_ENG = "vsvvvv"
+HM_LAG = 4
+DX0 = 13
+DW = [19, 23, 27]
+DX1 = 28
+OUT_BUFS = 10
+TAIL_V = 25
+
+
+def tile_binary_hinge_backward_s8_kernel(tc, x, wb, c, r, v_words, v_scales, out_0, out_1):
+    nc = tc.nc
+    with ExitStack() as ctx:
+        keep = ctx.enter_context(tc.tile_pool(name="keep", bufs=1))
+        work = ctx.enter_context(tc.tile_pool(name="work", bufs=3))
+        psum = ctx.enter_context(tc.psum_pool(name="psum", bufs=8))
+        ctx.enter_context(tc.manual_schedule())
+
+        def quantised(name, width):
+            codes = keep.tile([P, width], U32, name=name + "_codes", align_bytes=64)
+            scales = keep.tile([P, width], U8, name=name + "_scales", align_bytes=64)
+            return codes, scales
+
+        def quantise(pair, cols, src):
+            nc.vector.quantize_mx(out=pair[0][:, cols].bitcast(FP8X4), scales=pair[1][:, cols], in_=src)
+
+        def interleave(copy, dst, src):
+            copy(out=dst.rearrange("p (c i t) -> p c t i", i=4, t=PACK), in_=src.rearrange("p t (c i) -> p c t i", i=4))
+
+        ident = keep.tile([P, P], F32, name="ident")
+        make_identity(nc, ident[:])
+        v_plane = keep.tile([P, J * K], U8, name="v_plane", align_bytes=64)
+        nc.vector.memset(v_plane[:].bitcast(I32), 0)
+
+        x_rows = x.rearrange("(g p t) k -> g p t k", p=P, t=PACK)
+        c_rows = c.rearrange("(g p t) n -> g p t n", p=P, t=PACK)
+        w_rows = wb.rearrange("(a p t) n -> a p t n", p=P, t=PACK)
+        dx_rows = out_0.rearrange("(g p t) k -> g p t k", p=P, t=PACK)
+
+        x_sb = [keep.tile([P, PACK * K], BF16, name="x_sb%d" % g) for g in range(G)]
+        w_sb = {(a, j): keep.tile([P, PACK, PASS], BF16, name="w_sb%d%d" % (a, j)) for a in range(A) for j in range(J)}
+        c_sb = {(g, j): keep.tile([P, PACK, PASS], BF16, name="c_sb%d%d" % (g, j)) for g in range(G) for j in range(J)}
+        r_sb = keep.tile([P, G, PACK], BF16, name="r_sb")
+        v_sb = keep.tile([P, J, 2 * K], U8, name="v_sb", align_bytes=64)
+
+        def load_x(g, t0, t1):
+            nc.sync.dma_start(out=x_sb[g][:, t0 * K : t1 * K].rearrange("p (t k) -> p t k", k=K), in_=x_rows[g][:, t0:t1, :])
+
+        def load_w(a, j):
+            nc.sync.dma_start(out=w_sb[a, j][:], in_=w_rows[a][:, :, j * PASS : (j + 1) * PASS])
+
+        def load_c(g, j, t0, t1):
+            nc.sync.dma_start(out=c_sb[g, j][:, t0:t1, :], in_=c_rows[g][:, t0:t1, j * PASS : (j + 1) * PASS])
+
+        load_x(0, 0, 2)
+        load_w(0, 0)
+        load_w(1, 0)
+        load_c(0, 0, 0, 2)
+        nc.sync.dma_start(out=r_sb[:], in_=r.rearrange("(g p t) -> p g t", p=P, t=PACK))
+        load_x(0, 2, 4)
+        load_w(0, 1)
+        load_c(0, 0, 2, 4)
+        load_w(1, 1)
+        load_c(0, 1, 0, 4)
+        load_w(0, 2)
+        load_w(1, 2)
+        load_c(0, 2, 0, 4)
+        load_x(1, 0, 2)
+        load_x(1, 2, 4)
+        nc.sync.dma_start(out=v_sb[:].bitcast(I32), in_=v_words.rearrange("j p b -> p j b").bitcast(I32))
+        for q in range(4):
+            nc.sync.dma_start(
+                out=v_plane[32 * q : 32 * q + 4, :].rearrange("p (j k) -> p j k", j=J).bitcast(I32),
+                in_=v_scales[:, 4 * q : 4 * q + 4, :].rearrange("j s k -> s j k").bitcast(I32),
+            )
+        for j in range(J):
+            load_c(1, j, 0, 4)
+
+        xk = {(g, h): quantised("xk%d%d" % (g, h), 2 * A * P) for g in range(G) for h in range(2)}
+        xm = {(g, h): quantised("xm%d%d" % (g, h), PASS) for g in range(G) for h in range(2)}
+        wq = {(a, j): quantised("wq%d%d" % (a, j), PASS) for a in range(A) for j in range(J)}
+        hm = {u: quantised("hm%d%d" % u, PASS) for u in UNITS}
+        hn = {(g, j, h): quantised("hn%d%d%d" % (g, j, h), 2 * P) for g, j in UNITS for h in range(2)}
+        live = {}
+
+        def bank(key):
+            live[key] = psum.tile([P, PASS], F32, name="bank_%s" % "".join(map(str, key)), tag="bank")
+            return live[key]
+
+        def x_turn(g, t):
+            b = bank(("xt", g, t))
+            words = x_sb[g][:, t * K : (t + 1) * K].bitcast(F32)
+            for a in range(A):
+                for u in range(2):
+                    s = 2 * a + u
+                    nc.tensor.transpose(b[:, s * P : (s + 1) * P], words[:, 256 * a + u : 256 * (a + 1) : 2], ident[:])
+
+        def x_out(g, t, copy):
+            if t % 2 == 0:
+                live["xg", g, t // 2] = work.tile([P, 2048], BF16, name="xg", tag="stage", bufs=6, align_bytes=64)
+            dst = live["xg", g, t // 2][:, (t % 2) * 1024 : (t % 2 + 1) * 1024].bitcast(F32)
+            copy(out=dst.rearrange("p (a m u) -> p a m u", a=A, u=2),
+                           in_=live["xt", g, t][:].rearrange("p (a u m) -> p a m u", a=A, u=2))
+
+        def x_quant(g, h):
+            quantise(xk[g, h], slice(0, 512), live["xg", g, h][:])
+
+        def w_mix(a, j, copy, lo=0, hi=PASS):
+            if ("wg", a, j) not in live:
+                live["wg", a, j] = work.tile([P, 2048], BF16, name="wg", tag="stage", bufs=6, align_bytes=64)
+            interleave(copy, live["wg", a, j][:, 4 * lo : 4 * hi], w_sb[a, j][:, :, lo:hi])
+
+        def w_quant(a, j):
+            quantise(wq[a, j], slice(0, 512), live["wg", a, j][:])
+
+        def xm_mix(g, h, copy):
+            live["xmg", g, h] = work.tile([P, 2048], BF16, name="xmg", tag="stage", bufs=6, align_bytes=64)
+            interleave(copy, live["xmg", g, h][:], x_sb[g][:].rearrange("p (t k) -> p t k", t=PACK)[:, :, h * PASS : (h + 1) * PASS])
+
+        def xm_quant(g, h):
+            quantise(xm[g, h], slice(0, 512), live["xmg", g, h][:])
+
+        def z_mul(g, j, t):
+            b = bank(("z", g, j, t))
+            codes, scales = xk[g, t // 2]
+            for a in range(A):
+                cols = slice(((t % 2) * A + a) * P, ((t % 2) * A + a + 1) * P)
+                nc.tensor.matmul_mx(out=b[:], lhsT=codes[:, cols].bitcast(FP8X4), lhsT_scale=scales[:, cols],
+                                    rhs=wq[a, j][0][:].bitcast(FP8X4), rhs_scale=wq[a, j][1][:],
+                                    start=(a == 0), stop=(a == A - 1))
+
+        def shortfall(g, j, t):
+            d = work.tile([P, PASS], F32, name="d", tag="d", bufs=3)
+            live["d", g, j, t] = d
+            nc.vector.tensor_tensor(out=d[:].rearrange("p (u q e) -> p u q e", u=2, e=2),
+                                    in0=c_sb[g, j][:, t, :].rearrange("p (q u e) -> p u q e", u=2, e=2),
+                                    in1=live["z", g, j, t][:].rearrange("p (q u e) -> p u q e", u=2, e=2),
+                                    op=ALU.subtract)
+
+        def weigh(g, j, t):
+            if t == 0:
+                live["h", g, j] = work.tile([P, PACK * PASS], BF16, name="h", tag="h", bufs=6)
+            nc.vector.tensor_scalar(out=live["h", g, j][:, t * PASS : (t + 1) * PASS], in0=live["d", g, j, t][:],
+                                    scalar1=0.0, scalar2=r_sb[:, g, t : t + 1], op0=ALU.max, op1=ALU.mult)
+
+        def h_turn(g, j, h):
+            b = bank(("ht", g, j, h))
+            words = live["h", g, j][:].bitcast(F32)
+            for s in range(4):
+                w0 = (4 * h + s) * P
+                nc.tensor.transpose(b[:, s * P : (s + 1) * P], words[:, w0 : w0 + P], ident[:])
+
+        def h_out(g, j, h, copy):
+            live["hg", g, j, h] = work.tile([P, 1024], BF16, name="hg", tag="hg", bufs=4, align_bytes=64)
+            copy(out=live["hg", g, j, h][:].bitcast(F32).rearrange("p (t m u) -> p t m u", t=2, u=2),
+                           in_=live["ht", g, j, h][:].rearrange("p (t u m) -> p t m u", t=2, u=2))
+
+        def hn_quant(g, j, h):
+            quantise(hn[g, j, h], slice(0, 256), live["hg", g, j, h][:])
+
+        def hm_mix(g, j, copy):
+            live["hmg", g, j] = work.tile([P, 2048], BF16, name="hmg", tag="stage", bufs=6, align_bytes=64)
+            interleave(copy, live["hmg", g, j][:], live["h", g, j][:].rearrange("p (t n) -> p t n", t=PACK))
+
+        def hm_quant(g, j):
+            quantise(hm[g, j], slice(0, 512), live["hmg", g, j][:])
+
+        def dx_mul(g, t, kc):
+            b = bank(("dx", g, t, kc))
+            cols = slice((t % 2) * P, (t % 2 + 1) * P)
+            for j in range(J):
+                codes, scales = hn[g, j, t // 2]
+                nc.tensor.matmul_mx(out=b[:], lhsT=codes[:, cols].bitcast(FP8X4), lhsT_scale=scales[:, cols],
+                                    rhs=v_sb[:, j, kc * 1024 : (kc + 1) * 1024].bitcast(FP4X4),
+                                    rhs_scale=v_plane[:, j * K + kc * PASS : j * K + (kc + 1) * PASS],
+                                    start=(j == 0), stop=(j == J - 1))
+
+        def dx_out(g, t, kc, copy):
+            res = work.tile([P, PASS], F32, name="res", tag="res", bufs=OUT_BUFS)
+            copy(out=res[:], in_=live["dx", g, t, kc][:])
+            nc.sync.dma_start(out=dx_rows[g][:, t, kc * PASS : (kc + 1) * PASS], in_=res[:])
+
+        def dw_mul(kt, j):
+            b = bank(("dw", kt, j))
+            cols = slice((kt % 4) * P, (kt % 4 + 1) * P)
+            for g in range(G):
+                codes, scales = xm[g, kt // 4]
+                nc.tensor.matmul_mx(out=b[:], lhsT=codes[:, cols].bitcast(FP8X4), lhsT_scale=scales[:, cols],
+                                    rhs=hm[g, j][0][:].bitcast(FP8X4), rhs_scale=hm[g, j][1][:],
+                                    start=(g == 0), stop=(g == G - 1))
+
+        def dw_out(kt, j, copy):
+            res = work.tile([P, PASS], F32, name="res", tag="res", bufs=OUT_BUFS)
+            copy(out=res[:].rearrange("p (q u e) -> p q u e", u=2, e=2),
+                 in_=live["dw", kt, j][:].rearrange("p (u q e) -> p q u e", u=2, e=2))
+            nc.sync.dma_start(out=out_1[kt * P : (kt + 1) * P, j * PASS : (j + 1) * PASS], in_=res[:])
+
+        vec, sca = nc.vector.tensor_copy, nc.scalar.copy
+        x_turn(0, 0)
+        x_turn(0, 1)
+        x_out(0, 0, sca)
+        w_mix(0, 0, vec)
+        x_out(0, 1, sca)
+        w_mix(1, 0, vec, 0, SPLIT)
+        w_mix(1, 0, sca, SPLIT, PASS)
+        w_quant(0, 0)
+        x_quant(0, 0)
+        w_quant(1, 0)
+
+        plan = {}
+
+        def at(step, fn, *args):
+            plan.setdefault(step, []).append((fn, args))
+
+        cells = [(g, j, t) for g, j in UNITS for t in range(PACK)]
+        for i, cell in enumerate(cells):
+            at(i, shortfall, *cell)
+        for i, cell in enumerate(cells):
+            at(i + 1, weigh, *cell)
+        at(0, x_quant, 0, 1)
+        for i, cell in enumerate(cells):
+            at(i - AHEAD, z_mul, *cell)
+        for t in (2, 3):
+            at(-1, x_turn, 0, t)
+            at(-1, x_out, 0, t, sca)
+        at(-1, w_mix, 0, 1, vec)
+        at(0, w_mix, 1, 1, sca)
+        at(1, w_quant, 0, 1)
+        at(1, w_quant, 1, 1)
+        at(1, w_mix, 0, 2, sca)
+        at(3, w_mix, 1, 2, sca, W12, PASS)
+        at(4, w_mix, 1, 2, vec, 0, W12)
+        at(4, w_quant, 0, 2)
+        at(5, w_quant, 1, 2)
+        for t in range(PACK):
+            at(X1_STEP + t // 2, x_turn, 1, t)
+            at(X1_STEP + t // 2, x_out, 1, t, sca)
+        for h in range(2):
+            at(X1_STEP + 2 + 2 * h, x_quant, 1, h)
+        for n, (j, h) in enumerate([(j, h) for j in range(J) for h in range(2)]):
+            at(HT0[n], h_turn, 0, j, h)
+            at(HT0[n], h_out, 0, j, h, sca)
+            at(HT0[n] + 1, hn_quant, 0, j, h)
+            at(HT1[n], h_turn, 1, j, h)
+            at(HT1[n], h_out, 1, j, h, sca)
+            at(HT1[n] + 1, hn_quant, 1, j, h)
+        for n, (h, g) in enumerate(X0_ORDER):
+            at(X0_STEPS[n], xm_mix, g, h, sca if X0_ENG[n] == "s" else vec)
+            at(X0_STEPS[n] + X0_LAG, xm_quant, g, h)
+        for n, (g, j) in enumerate(UNITS):
+            at(HM[n], hm_mix, g, j, sca if HM_ENG[n] == "s" else vec)
+            at(HM[n] + (HM_LAG if HM_ENG[n] == "s" else 1), hm_quant, g, j)
+        outs = []
+        for n in range(8):
+            outs.append((DX0 + n, dx_mul, dx_out, (0, n // 2, n % 2)))
+        for j in range(J):
+            for n in range(8):
+                outs.append((DW[j] + n // 2, dw_mul, dw_out, (n, j)))
+        for n in range(8):
+            outs.append((DX1 + n // 2, dx_mul, dx_out, (1, n // 2, n % 2)))
+        for n, (step, mul, out, args) in enumerate(outs):
+            at(step, mul, *args)
+            at(step + 1, out, *args, vec if (step >= TAIL_V and n % 2 == 0) else sca)
+        for s in sorted(plan):
+            for fn, args in plan[s]:
+                fn(*args)

@@ -18,48 +18,27 @@ ALU = mybir.AluOpType
 P = 128
 PACK = 4
 PASS = P * PACK
-G = M // PASS
-A = K // PASS
-J = N // PASS
-UNITS = [(0, 0), (0, 1), (0, 2), (1, 0), (1, 1), (1, 2)]
+G, A, J = M // PASS, K // PASS, N // PASS
+RUN = 4
+TILES = G * J * PACK
+HALF = J * PACK
+
+SUBTRACT, SCALAR_MIX, WEIGH, VECTOR_SIDE, MARGINS, TURN, PRODUCT = range(7)
+
 AHEAD = 2
-SPLIT = 352
-W12 = 256
-X1_STEP = 7
-X0_ORDER = [(0, 0), (1, 0), (0, 1), (1, 1)]
-X0_STEPS = [6, 10, 12, 14]
-X0_ENG = "ssss"
-X0_LAG = 4
-HT0 = [4, 5, 8, 9, 11, 13]
-HT1 = [23, 23, 24, 24, 25, 26]
-HM = [15, 16, 23, 17, 21, 25]
-HM_ENG = "vsvvvv"
-HM_LAG = 4
-DX0 = 13
-DW = [19, 23, 27]
-DX1 = 28
-OUT_BUFS = 10
-TAIL_V = 25
+X_TURN = (0, 4)
+H_MIX = 8
+DW_START = 18
 
 
 def tile_binary_hinge_backward_s8_kernel(tc, x, wb, c, r, v_words, v_scales, out_0, out_1):
     nc = tc.nc
+    on_vector, on_scalar = nc.vector.tensor_copy, nc.scalar.copy
     with ExitStack() as ctx:
         keep = ctx.enter_context(tc.tile_pool(name="keep", bufs=1))
         work = ctx.enter_context(tc.tile_pool(name="work", bufs=3))
         psum = ctx.enter_context(tc.psum_pool(name="psum", bufs=8))
         ctx.enter_context(tc.manual_schedule())
-
-        def quantised(name, width):
-            codes = keep.tile([P, width], U32, name=name + "_codes", align_bytes=64)
-            scales = keep.tile([P, width], U8, name=name + "_scales", align_bytes=64)
-            return codes, scales
-
-        def quantise(pair, cols, src):
-            nc.vector.quantize_mx(out=pair[0][:, cols].bitcast(FP8X4), scales=pair[1][:, cols], in_=src)
-
-        def interleave(copy, dst, src):
-            copy(out=dst.rearrange("p (c i t) -> p c t i", i=4, t=PACK), in_=src.rearrange("p t (c i) -> p c t i", i=4))
 
         ident = keep.tile([P, P], F32, name="ident")
         make_identity(nc, ident[:])
@@ -72,229 +51,214 @@ def tile_binary_hinge_backward_s8_kernel(tc, x, wb, c, r, v_words, v_scales, out
         dx_rows = out_0.rearrange("(g p t) k -> g p t k", p=P, t=PACK)
 
         x_sb = [keep.tile([P, PACK * K], BF16, name="x_sb%d" % g) for g in range(G)]
-        w_sb = {(a, j): keep.tile([P, PACK, PASS], BF16, name="w_sb%d%d" % (a, j)) for a in range(A) for j in range(J)}
-        c_sb = {(g, j): keep.tile([P, PACK, PASS], BF16, name="c_sb%d%d" % (g, j)) for g in range(G) for j in range(J)}
         r_sb = keep.tile([P, G, PACK], BF16, name="r_sb")
         v_sb = keep.tile([P, J, 2 * K], U8, name="v_sb", align_bytes=64)
+        w_sb, c_sb = {}, {}
 
         def load_x(g, t0, t1):
             nc.sync.dma_start(out=x_sb[g][:, t0 * K : t1 * K].rearrange("p (t k) -> p t k", k=K), in_=x_rows[g][:, t0:t1, :])
 
         def load_w(a, j):
+            w_sb[a, j] = work.tile([P, PACK, PASS], BF16, name="w_sb", tag="row", bufs=A * J)
             nc.sync.dma_start(out=w_sb[a, j][:], in_=w_rows[a][:, :, j * PASS : (j + 1) * PASS])
 
-        def load_c(g, j, t0, t1):
-            nc.sync.dma_start(out=c_sb[g, j][:, t0:t1, :], in_=c_rows[g][:, t0:t1, j * PASS : (j + 1) * PASS])
+        def load_c(g, j0, j1):
+            tile = keep.tile([P, PACK, (j1 - j0) * PASS], BF16, name="c_sb%d%d" % (g, j0))
+            nc.sync.dma_start(out=tile[:], in_=c_rows[g][:, :, j0 * PASS : j1 * PASS])
+            for j in range(j0, j1):
+                c_sb[g, j] = tile[:, :, (j - j0) * PASS : (j - j0 + 1) * PASS]
 
-        load_x(0, 0, 2)
         load_w(0, 0)
-        load_w(1, 0)
-        load_c(0, 0, 0, 2)
-        nc.sync.dma_start(out=r_sb[:], in_=r.rearrange("(g p t) -> p g t", p=P, t=PACK))
+        load_x(0, 0, 2)
         load_x(0, 2, 4)
+        nc.sync.dma_start(out=r_sb[:], in_=r.rearrange("(g p t) -> p g t", p=P, t=PACK))
+        load_w(1, 0)
+        load_c(0, 0, 1)
         load_w(0, 1)
-        load_c(0, 0, 2, 4)
         load_w(1, 1)
-        load_c(0, 1, 0, 4)
+        load_x(1, 0, 4)
         load_w(0, 2)
+        load_c(0, 1, 2)
         load_w(1, 2)
-        load_c(0, 2, 0, 4)
-        load_x(1, 0, 2)
-        load_x(1, 2, 4)
+        load_c(0, 2, 3)
+        load_c(1, 0, 1)
         nc.sync.dma_start(out=v_sb[:].bitcast(I32), in_=v_words.rearrange("j p b -> p j b").bitcast(I32))
         for q in range(4):
             nc.sync.dma_start(
-                out=v_plane[32 * q : 32 * q + 4, :].rearrange("p (j k) -> p j k", j=J).bitcast(I32),
+                out=v_plane[32 * q : 32 * q + 4, :].rearrange("s (j k) -> s j k", j=J).bitcast(I32),
                 in_=v_scales[:, 4 * q : 4 * q + 4, :].rearrange("j s k -> s j k").bitcast(I32),
             )
-        for j in range(J):
-            load_c(1, j, 0, 4)
+        load_c(1, 1, 3)
 
-        xk = {(g, h): quantised("xk%d%d" % (g, h), 2 * A * P) for g in range(G) for h in range(2)}
-        xm = {(g, h): quantised("xm%d%d" % (g, h), PASS) for g in range(G) for h in range(2)}
-        wq = {(a, j): quantised("wq%d%d" % (a, j), PASS) for a in range(A) for j in range(J)}
-        hm = {u: quantised("hm%d%d" % u, PASS) for u in UNITS}
-        hn = {(g, j, h): quantised("hn%d%d%d" % (g, j, h), 2 * P) for g, j in UNITS for h in range(2)}
+        def quantised(name, width):
+            codes = keep.tile([P, width], U32, name=name + "_codes", align_bytes=64)
+            scales = keep.tile([P, width], U8, name=name + "_scales", align_bytes=64)
+            return codes, scales
+
+        x_by_k = {(g, t): quantised("xk%d%d" % (g, t), A * P) for g in range(G) for t in range(PACK)}
+        x_by_m = {(g, a): quantised("xm%d%d" % (g, a), PASS) for g in range(G) for a in range(A)}
+        w_by_k = {(a, j): quantised("wq%d%d" % (a, j), PASS) for a in range(A) for j in range(J)}
+        h_by_m = {(g, j): quantised("hm%d%d" % (g, j), PASS) for g in range(G) for j in range(J)}
+        h_by_n = {(g, j, pair): quantised("hn%d%d%d" % (g, j, pair), 2 * P) for g in range(G) for j in range(J) for pair in range(2)}
         live = {}
 
-        def bank(key):
-            live[key] = psum.tile([P, PASS], F32, name="bank_%s" % "".join(map(str, key)), tag="bank")
-            return live[key]
+        def quantise(operand, key):
+            nc.vector.quantize_mx(out=operand[0][:].bitcast(FP8X4), scales=operand[1][:], in_=live[key][:])
+
+        def multiply(key, passes):
+            live[key] = psum.tile([P, PASS], F32, name="bank", tag="bank")
+            for n, (lhsT, lhsT_scale, rhs, rhs_scale) in enumerate(passes):
+                nc.tensor.matmul_mx(out=live[key][:], lhsT=lhsT, lhsT_scale=lhsT_scale, rhs=rhs, rhs_scale=rhs_scale,
+                                    start=(n == 0), stop=(n == len(passes) - 1))
+
+        def columns(operand, first, width):
+            return operand[0][:, first : first + width].bitcast(FP8X4), operand[1][:, first : first + width]
+
+        def mix(copy, key, rows, tag, bufs):
+            live[key] = work.tile([P, PACK * PASS], BF16, name=tag, tag=tag, bufs=bufs, align_bytes=64)
+            copy(out=live[key][:].rearrange("p (c i t) -> p c t i", i=RUN, t=PACK), in_=rows.rearrange("p t (c i) -> p c t i", i=RUN))
+
+        def turn(key, blocks):
+            bank = psum.tile([P, PASS], F32, name="bank", tag="bank")
+            for n, block in enumerate(blocks):
+                nc.tensor.transpose(bank[:, n * P : (n + 1) * P], block, ident[:])
+            live[key] = work.tile([P, 2 * PASS], BF16, name="turned", tag="turned", bufs=8, align_bytes=64)
+            on_scalar(out=live[key][:].bitcast(F32).rearrange("p (b m u) -> p b m u", b=2, u=2),
+                      in_=bank[:].rearrange("p (b u m) -> p b m u", b=2, u=2))
 
         def x_turn(g, t):
-            b = bank(("xt", g, t))
             words = x_sb[g][:, t * K : (t + 1) * K].bitcast(F32)
-            for a in range(A):
-                for u in range(2):
-                    s = 2 * a + u
-                    nc.tensor.transpose(b[:, s * P : (s + 1) * P], words[:, 256 * a + u : 256 * (a + 1) : 2], ident[:])
+            turn(("x turned", g, t), [words[:, 2 * P * a + u : 2 * P * (a + 1) : 2] for a in range(A) for u in range(2)])
 
-        def x_out(g, t, copy):
-            if t % 2 == 0:
-                live["xg", g, t // 2] = work.tile([P, 2048], BF16, name="xg", tag="stage", bufs=6, align_bytes=64)
-            dst = live["xg", g, t // 2][:, (t % 2) * 1024 : (t % 2 + 1) * 1024].bitcast(F32)
-            copy(out=dst.rearrange("p (a m u) -> p a m u", a=A, u=2),
-                           in_=live["xt", g, t][:].rearrange("p (a u m) -> p a m u", a=A, u=2))
+        def x_turned_quantise(g, t):
+            quantise(x_by_k[g, t], ("x turned", g, t))
 
-        def x_quant(g, h):
-            quantise(xk[g, h], slice(0, 512), live["xg", g, h][:])
+        def x_mix(copy, g, a):
+            rows = x_sb[g][:].rearrange("p (t k) -> p t k", t=PACK)[:, :, a * PASS : (a + 1) * PASS]
+            mix(copy, ("x mixed", g, a), rows, "x_mixed", 3)
 
-        def w_mix(a, j, copy, lo=0, hi=PASS):
-            if ("wg", a, j) not in live:
-                live["wg", a, j] = work.tile([P, 2048], BF16, name="wg", tag="stage", bufs=6, align_bytes=64)
-            interleave(copy, live["wg", a, j][:, 4 * lo : 4 * hi], w_sb[a, j][:, :, lo:hi])
+        def x_mixed_quantise(g, a):
+            quantise(x_by_m[g, a], ("x mixed", g, a))
 
-        def w_quant(a, j):
-            quantise(wq[a, j], slice(0, 512), live["wg", a, j][:])
+        def w_mix(copy, a, j):
+            mix(copy, ("w mixed", a, j), w_sb[a, j][:], "mixed", 4)
 
-        def xm_mix(g, h, copy):
-            live["xmg", g, h] = work.tile([P, 2048], BF16, name="xmg", tag="stage", bufs=6, align_bytes=64)
-            interleave(copy, live["xmg", g, h][:], x_sb[g][:].rearrange("p (t k) -> p t k", t=PACK)[:, :, h * PASS : (h + 1) * PASS])
+        def w_quantise(a, j):
+            quantise(w_by_k[a, j], ("w mixed", a, j))
 
-        def xm_quant(g, h):
-            quantise(xm[g, h], slice(0, 512), live["xmg", g, h][:])
+        def margins(g, j, t):
+            multiply(("z", g, j, t), [columns(x_by_k[g, t], a * P, P) + columns(w_by_k[a, j], 0, PASS) for a in range(A)])
 
-        def z_mul(g, j, t):
-            b = bank(("z", g, j, t))
-            codes, scales = xk[g, t // 2]
-            for a in range(A):
-                cols = slice(((t % 2) * A + a) * P, ((t % 2) * A + a + 1) * P)
-                nc.tensor.matmul_mx(out=b[:], lhsT=codes[:, cols].bitcast(FP8X4), lhsT_scale=scales[:, cols],
-                                    rhs=wq[a, j][0][:].bitcast(FP8X4), rhs_scale=wq[a, j][1][:],
-                                    start=(a == 0), stop=(a == A - 1))
-
-        def shortfall(g, j, t):
-            d = work.tile([P, PASS], F32, name="d", tag="d", bufs=3)
-            live["d", g, j, t] = d
-            nc.vector.tensor_tensor(out=d[:].rearrange("p (u q e) -> p u q e", u=2, e=2),
+        def subtract(g, j, t):
+            live["d", g, j, t] = work.tile([P, PASS], F32, name="d", tag="d")
+            nc.vector.tensor_tensor(out=live["d", g, j, t][:].rearrange("p (u q e) -> p u q e", u=2, e=2),
                                     in0=c_sb[g, j][:, t, :].rearrange("p (q u e) -> p u q e", u=2, e=2),
                                     in1=live["z", g, j, t][:].rearrange("p (q u e) -> p u q e", u=2, e=2),
                                     op=ALU.subtract)
 
         def weigh(g, j, t):
             if t == 0:
-                live["h", g, j] = work.tile([P, PACK * PASS], BF16, name="h", tag="h", bufs=6)
+                live["h", g, j] = work.tile([P, PACK * PASS], BF16, name="h", tag="h", bufs=G * J)
             nc.vector.tensor_scalar(out=live["h", g, j][:, t * PASS : (t + 1) * PASS], in0=live["d", g, j, t][:],
                                     scalar1=0.0, scalar2=r_sb[:, g, t : t + 1], op0=ALU.max, op1=ALU.mult)
 
-        def h_turn(g, j, h):
-            b = bank(("ht", g, j, h))
+        def h_turn(g, j, pair):
             words = live["h", g, j][:].bitcast(F32)
-            for s in range(4):
-                w0 = (4 * h + s) * P
-                nc.tensor.transpose(b[:, s * P : (s + 1) * P], words[:, w0 : w0 + P], ident[:])
+            turn(("h turned", g, j, pair), [words[:, (4 * pair + n) * P : (4 * pair + n + 1) * P] for n in range(4)])
 
-        def h_out(g, j, h, copy):
-            live["hg", g, j, h] = work.tile([P, 1024], BF16, name="hg", tag="hg", bufs=4, align_bytes=64)
-            copy(out=live["hg", g, j, h][:].bitcast(F32).rearrange("p (t m u) -> p t m u", t=2, u=2),
-                           in_=live["ht", g, j, h][:].rearrange("p (t u m) -> p t m u", t=2, u=2))
+        def h_turned_quantise(g, j, pair):
+            quantise(h_by_n[g, j, pair], ("h turned", g, j, pair))
 
-        def hn_quant(g, j, h):
-            quantise(hn[g, j, h], slice(0, 256), live["hg", g, j, h][:])
+        def h_mix(copy, g, j):
+            mix(copy, ("h mixed", g, j), live["h", g, j][:].rearrange("p (t n) -> p t n", t=PACK), "mixed", 4)
 
-        def hm_mix(g, j, copy):
-            live["hmg", g, j] = work.tile([P, 2048], BF16, name="hmg", tag="stage", bufs=6, align_bytes=64)
-            interleave(copy, live["hmg", g, j][:], live["h", g, j][:].rearrange("p (t n) -> p t n", t=PACK))
+        def h_mixed_quantise(g, j):
+            quantise(h_by_m[g, j], ("h mixed", g, j))
 
-        def hm_quant(g, j):
-            quantise(hm[g, j], slice(0, 512), live["hmg", g, j][:])
+        def dx_product(copy, g, t, a):
+            multiply("dx", [columns(h_by_n[g, j, t // 2], t % 2 * P, P)
+                            + (v_sb[:, j, 2 * a * PASS : 2 * (a + 1) * PASS].bitcast(FP4X4),
+                               v_plane[:, j * K + a * PASS : j * K + (a + 1) * PASS]) for j in range(J)])
+            if a == 0:
+                live["dx row", g, t] = work.tile([P, K], F32, name="dx_row", tag="row", bufs=A * J)
+            row, cols = live["dx row", g, t], slice(a * PASS, (a + 1) * PASS)
+            copy(out=row[:, cols], in_=live["dx"][:])
+            if (g, t // 2) == (G - 1, 1):
+                nc.sync.dma_start(out=dx_rows[g][:, t, cols], in_=row[:, cols])
+            elif a == A - 1:
+                nc.sync.dma_start(out=dx_rows[g][:, t, :], in_=row[:])
 
-        def dx_mul(g, t, kc):
-            b = bank(("dx", g, t, kc))
-            cols = slice((t % 2) * P, (t % 2 + 1) * P)
-            for j in range(J):
-                codes, scales = hn[g, j, t // 2]
-                nc.tensor.matmul_mx(out=b[:], lhsT=codes[:, cols].bitcast(FP8X4), lhsT_scale=scales[:, cols],
-                                    rhs=v_sb[:, j, kc * 1024 : (kc + 1) * 1024].bitcast(FP4X4),
-                                    rhs_scale=v_plane[:, j * K + kc * PASS : j * K + (kc + 1) * PASS],
-                                    start=(j == 0), stop=(j == J - 1))
+        def dw_product(copy, kt, j):
+            multiply("dw", [columns(x_by_m[g, kt // PACK], kt % PACK * P, P) + columns(h_by_m[g, j], 0, PASS) for g in range(G)])
+            block = work.tile([P, PASS], F32, name="dw_block", tag="dw_block", bufs=10)
+            copy(out=block[:].rearrange("p (q u e) -> p q u e", u=2, e=2),
+                 in_=live["dw"][:].rearrange("p (u q e) -> p q u e", u=2, e=2))
+            nc.sync.dma_start(out=out_1[kt * P : (kt + 1) * P, j * PASS : (j + 1) * PASS], in_=block[:])
 
-        def dx_out(g, t, kc, copy):
-            res = work.tile([P, PASS], F32, name="res", tag="res", bufs=OUT_BUFS)
-            copy(out=res[:], in_=live["dx", g, t, kc][:])
-            nc.sync.dma_start(out=dx_rows[g][:, t, kc * PASS : (kc + 1) * PASS], in_=res[:])
+        w_mix(on_scalar, 0, 0)
+        x_mix(on_vector, 0, 0)
+        w_quantise(0, 0)
+        for t in range(PACK - 1):
+            x_turn(0, t)
+        w_mix(on_vector, 1, 0)
+        x_mixed_quantise(0, 0)
+        w_quantise(1, 0)
+        x_turned_quantise(0, 0)
+        x_mix(on_scalar, 0, 1)
+        x_turn(0, PACK - 1)
+        w_mix(on_vector, 0, 1)
+        for t in range(1, PACK):
+            x_turned_quantise(0, t)
+        x_mixed_quantise(0, 1)
 
-        def dw_mul(kt, j):
-            b = bank(("dw", kt, j))
-            cols = slice((kt % 4) * P, (kt % 4 + 1) * P)
-            for g in range(G):
-                codes, scales = xm[g, kt // 4]
-                nc.tensor.matmul_mx(out=b[:], lhsT=codes[:, cols].bitcast(FP8X4), lhsT_scale=scales[:, cols],
-                                    rhs=hm[g, j][0][:].bitcast(FP8X4), rhs_scale=hm[g, j][1][:],
-                                    start=(g == 0), stop=(g == G - 1))
+        due = {}
 
-        def dw_out(kt, j, copy):
-            res = work.tile([P, PASS], F32, name="res", tag="res", bufs=OUT_BUFS)
-            copy(out=res[:].rearrange("p (q u e) -> p q u e", u=2, e=2),
-                 in_=live["dw", kt, j][:].rearrange("p (u q e) -> p q u e", u=2, e=2))
-            nc.sync.dma_start(out=out_1[kt * P : (kt + 1) * P, j * PASS : (j + 1) * PASS], in_=res[:])
+        def at(step, phase, job, *args):
+            due.setdefault((step, phase), []).append((job, args))
 
-        vec, sca = nc.vector.tensor_copy, nc.scalar.copy
-        x_turn(0, 0)
-        x_turn(0, 1)
-        x_out(0, 0, sca)
-        w_mix(0, 0, vec)
-        x_out(0, 1, sca)
-        w_mix(1, 0, vec, 0, SPLIT)
-        w_mix(1, 0, sca, SPLIT, PASS)
-        w_quant(0, 0)
-        x_quant(0, 0)
-        w_quant(1, 0)
+        tiles = [(g, j, t) for g in range(G) for j in range(J) for t in range(PACK)]
+        for i, tile_i in enumerate(tiles):
+            at(i - AHEAD, MARGINS, margins, *tile_i)
+            at(i, SUBTRACT, subtract, *tile_i)
+            at(i + 1, WEIGH, weigh, *tile_i)
 
-        plan = {}
-
-        def at(step, fn, *args):
-            plan.setdefault(step, []).append((fn, args))
-
-        cells = [(g, j, t) for g, j in UNITS for t in range(PACK)]
-        for i, cell in enumerate(cells):
-            at(i, shortfall, *cell)
-        for i, cell in enumerate(cells):
-            at(i + 1, weigh, *cell)
-        at(0, x_quant, 0, 1)
-        for i, cell in enumerate(cells):
-            at(i - AHEAD, z_mul, *cell)
-        for t in (2, 3):
-            at(-1, x_turn, 0, t)
-            at(-1, x_out, 0, t, sca)
-        at(-1, w_mix, 0, 1, vec)
-        at(0, w_mix, 1, 1, sca)
-        at(1, w_quant, 0, 1)
-        at(1, w_quant, 1, 1)
-        at(1, w_mix, 0, 2, sca)
-        at(3, w_mix, 1, 2, sca, W12, PASS)
-        at(4, w_mix, 1, 2, vec, 0, W12)
-        at(4, w_quant, 0, 2)
-        at(5, w_quant, 1, 2)
+        at(-1, SCALAR_MIX, w_mix, on_scalar, 1, 1)
+        for a in range(A):
+            at(1, SCALAR_MIX, w_mix, on_scalar, a, 2)
+            for j in range(1, J):
+                at(PACK * j - AHEAD - 1 + a, VECTOR_SIDE, w_quantise, a, j)
         for t in range(PACK):
-            at(X1_STEP + t // 2, x_turn, 1, t)
-            at(X1_STEP + t // 2, x_out, 1, t, sca)
-        for h in range(2):
-            at(X1_STEP + 2 + 2 * h, x_quant, 1, h)
-        for n, (j, h) in enumerate([(j, h) for j in range(J) for h in range(2)]):
-            at(HT0[n], h_turn, 0, j, h)
-            at(HT0[n], h_out, 0, j, h, sca)
-            at(HT0[n] + 1, hn_quant, 0, j, h)
-            at(HT1[n], h_turn, 1, j, h)
-            at(HT1[n], h_out, 1, j, h, sca)
-            at(HT1[n] + 1, hn_quant, 1, j, h)
-        for n, (h, g) in enumerate(X0_ORDER):
-            at(X0_STEPS[n], xm_mix, g, h, sca if X0_ENG[n] == "s" else vec)
-            at(X0_STEPS[n] + X0_LAG, xm_quant, g, h)
-        for n, (g, j) in enumerate(UNITS):
-            at(HM[n], hm_mix, g, j, sca if HM_ENG[n] == "s" else vec)
-            at(HM[n] + (HM_LAG if HM_ENG[n] == "s" else 1), hm_quant, g, j)
-        outs = []
-        for n in range(8):
-            outs.append((DX0 + n, dx_mul, dx_out, (0, n // 2, n % 2)))
+            at(X_TURN[t // 2], TURN, x_turn, 1, t)
+            at(HALF + t - AHEAD - 2, VECTOR_SIDE, x_turned_quantise, 1, t)
+
+        for pair in range(2):
+            last_weighed = HALF - 2 + 2 * pair
+            for j in range(J):
+                at(min(PACK * j + PACK, last_weighed) + 1, TURN, h_turn, 0, j, pair)
+                at(last_weighed + 3, VECTOR_SIDE, h_turned_quantise, 0, j, pair)
+                at(HALF + last_weighed + 1, TURN, h_turn, 1, j, pair)
+                at(TILES + 2 + pair, VECTOR_SIDE, h_turned_quantise, 1, j, pair)
+            for n in range(2 * A):
+                at(last_weighed + 3 + n, PRODUCT, dx_product, on_scalar, 0, 2 * pair + n // A, n % A)
+
+        for a in range(A):
+            at(HALF + 2 * a, SCALAR_MIX, x_mix, on_scalar, 1, a)
+            at(DW_START - 2 + 2 * a, VECTOR_SIDE, x_mixed_quantise, 1, a)
+        at(H_MIX, SCALAR_MIX, h_mix, on_scalar, 0, 0)
+        at(HALF + PACK, SCALAR_MIX, h_mix, on_scalar, 0, 1)
+        at(TILES, VECTOR_SIDE, h_mix, on_vector, 0, 2)
         for j in range(J):
-            for n in range(8):
-                outs.append((DW[j] + n // 2, dw_mul, dw_out, (n, j)))
-        for n in range(8):
-            outs.append((DX1 + n // 2, dx_mul, dx_out, (1, n // 2, n % 2)))
-        for n, (step, mul, out, args) in enumerate(outs):
-            at(step, mul, *args)
-            at(step + 1, out, *args, vec if (step >= TAIL_V and n % 2 == 0) else sca)
-        for s in sorted(plan):
-            for fn, args in plan[s]:
-                fn(*args)
+            weighed = HALF + PACK * j + PACK
+            at(weighed, VECTOR_SIDE, h_mix, on_vector, 1, j)
+            for g in range(G):
+                at(weighed + 1, VECTOR_SIDE, h_mixed_quantise, g, j)
+
+        products = [(dw_product, kt, j) for j in range(J) for kt in range(K // P)]
+        products = products + [(dx_product, 1, t, a) for t in range(PACK) for a in range(A)]
+        for n, (job, *args) in enumerate(products):
+            step = DW_START + n // 2
+            at(step, PRODUCT, job, on_vector if step > TILES + 3 and n % 2 == 0 else on_scalar, *args)
+
+        for key in sorted(due):
+            for job, args in due[key]:
+                job(*args)

@@ -26,7 +26,7 @@ HALF = J * PACK
 SUBTRACT, SCALAR_MIX, WEIGH, VECTOR_SIDE, MARGINS, TURN, PRODUCT = range(7)
 
 AHEAD = 2
-X_TURN = (0, 4)
+X_TURN = 5
 H_MIX = 8
 DW_START = 18
 
@@ -68,18 +68,17 @@ def tile_binary_hinge_backward_s8_kernel(tc, x, wb, c, r, v_words, v_scales, out
             for j in range(j0, j1):
                 c_sb[g, j] = tile[:, :, (j - j0) * PASS : (j - j0 + 1) * PASS]
 
-        load_w(0, 0)
         load_x(0, 0, 2)
+        load_w(0, 0)
         load_x(0, 2, 4)
-        nc.sync.dma_start(out=r_sb[:], in_=r.rearrange("(g p t) -> p g t", p=P, t=PACK))
         load_w(1, 0)
         load_c(0, 0, 1)
-        load_w(0, 1)
-        load_w(1, 1)
-        load_x(1, 0, 4)
-        load_w(0, 2)
+        nc.sync.dma_start(out=r_sb[:], in_=r.rearrange("(g p t) -> p g t", p=P, t=PACK))
+        for j in range(1, J):
+            for a in range(A):
+                load_w(a, j)
         load_c(0, 1, 2)
-        load_w(1, 2)
+        load_x(1, 0, 4)
         load_c(0, 2, 3)
         load_c(1, 0, 1)
         nc.sync.dma_start(out=v_sb[:].bitcast(I32), in_=v_words.rearrange("j p b -> p j b").bitcast(I32))
@@ -118,24 +117,24 @@ def tile_binary_hinge_backward_s8_kernel(tc, x, wb, c, r, v_words, v_scales, out
             live[key] = work.tile([P, PACK * PASS], BF16, name=tag, tag=tag, bufs=bufs, align_bytes=64)
             copy(out=live[key][:].rearrange("p (c i t) -> p c t i", i=RUN, t=PACK), in_=rows.rearrange("p t (c i) -> p c t i", i=RUN))
 
-        def turn(key, blocks):
+        def turn(copy, key, blocks):
             bank = psum.tile([P, PASS], F32, name="bank", tag="bank")
             for n, block in enumerate(blocks):
                 nc.tensor.transpose(bank[:, n * P : (n + 1) * P], block, ident[:])
-            live[key] = work.tile([P, 2 * PASS], BF16, name="turned", tag="turned", bufs=8, align_bytes=64)
-            on_scalar(out=live[key][:].bitcast(F32).rearrange("p (b m u) -> p b m u", b=2, u=2),
-                      in_=bank[:].rearrange("p (b u m) -> p b m u", b=2, u=2))
+            live[key] = work.tile([P, 2 * PASS], BF16, name="turned", tag="turned", bufs=9, align_bytes=64)
+            copy(out=live[key][:].bitcast(F32).rearrange("p (b m u) -> p b m u", b=2, u=2),
+                 in_=bank[:].rearrange("p (b u m) -> p b m u", b=2, u=2))
 
         def x_turn(g, t):
             words = x_sb[g][:, t * K : (t + 1) * K].bitcast(F32)
-            turn(("x turned", g, t), [words[:, 2 * P * a + u : 2 * P * (a + 1) : 2] for a in range(A) for u in range(2)])
+            turn(on_scalar, ("x turned", g, t), [words[:, 2 * P * a + u : 2 * P * (a + 1) : 2] for a in range(A) for u in range(2)])
 
         def x_turned_quantise(g, t):
             quantise(x_by_k[g, t], ("x turned", g, t))
 
         def x_mix(copy, g, a):
             rows = x_sb[g][:].rearrange("p (t k) -> p t k", t=PACK)[:, :, a * PASS : (a + 1) * PASS]
-            mix(copy, ("x mixed", g, a), rows, "x_mixed", 3)
+            mix(copy, ("x mixed", g, a), rows, "x_mixed", G * A)
 
         def x_mixed_quantise(g, a):
             quantise(x_by_m[g, a], ("x mixed", g, a))
@@ -162,9 +161,9 @@ def tile_binary_hinge_backward_s8_kernel(tc, x, wb, c, r, v_words, v_scales, out
             nc.vector.tensor_scalar(out=live["h", g, j][:, t * PASS : (t + 1) * PASS], in0=live["d", g, j, t][:],
                                     scalar1=0.0, scalar2=r_sb[:, g, t : t + 1], op0=ALU.max, op1=ALU.mult)
 
-        def h_turn(g, j, pair):
+        def h_turn(copy, g, j, pair):
             words = live["h", g, j][:].bitcast(F32)
-            turn(("h turned", g, j, pair), [words[:, (4 * pair + n) * P : (4 * pair + n + 1) * P] for n in range(4)])
+            turn(copy, ("h turned", g, j, pair), [words[:, (4 * pair + n) * P : (4 * pair + n + 1) * P] for n in range(4)])
 
         def h_turned_quantise(g, j, pair):
             quantise(h_by_n[g, j, pair], ("h turned", g, j, pair))
@@ -190,26 +189,23 @@ def tile_binary_hinge_backward_s8_kernel(tc, x, wb, c, r, v_words, v_scales, out
 
         def dw_product(copy, kt, j):
             multiply("dw", [columns(x_by_m[g, kt // PACK], kt % PACK * P, P) + columns(h_by_m[g, j], 0, PASS) for g in range(G)])
-            block = work.tile([P, PASS], F32, name="dw_block", tag="dw_block", bufs=10)
+            block = work.tile([P, PASS], F32, name="dw_block", tag="dw_block", bufs=8)
             copy(out=block[:].rearrange("p (q u e) -> p q u e", u=2, e=2),
                  in_=live["dw"][:].rearrange("p (u q e) -> p q u e", u=2, e=2))
             nc.sync.dma_start(out=out_1[kt * P : (kt + 1) * P, j * PASS : (j + 1) * PASS], in_=block[:])
 
-        w_mix(on_scalar, 0, 0)
-        x_mix(on_vector, 0, 0)
+        w_mix(on_vector, 0, 0)
+        for t in range(2):
+            x_turn(0, t)
         w_quantise(0, 0)
-        for t in range(PACK - 1):
+        for t in range(2):
+            x_turned_quantise(0, t)
+        x_mix(on_scalar, 0, 0)
+        for t in range(2, PACK):
             x_turn(0, t)
         w_mix(on_vector, 1, 0)
-        x_mixed_quantise(0, 0)
         w_quantise(1, 0)
-        x_turned_quantise(0, 0)
         x_mix(on_scalar, 0, 1)
-        x_turn(0, PACK - 1)
-        w_mix(on_vector, 0, 1)
-        for t in range(1, PACK):
-            x_turned_quantise(0, t)
-        x_mixed_quantise(0, 1)
 
         due = {}
 
@@ -222,28 +218,37 @@ def tile_binary_hinge_backward_s8_kernel(tc, x, wb, c, r, v_words, v_scales, out
             at(i, SUBTRACT, subtract, *tile_i)
             at(i + 1, WEIGH, weigh, *tile_i)
 
-        at(-1, SCALAR_MIX, w_mix, on_scalar, 1, 1)
-        for a in range(A):
-            at(1, SCALAR_MIX, w_mix, on_scalar, a, 2)
-            for j in range(1, J):
+        at(0, VECTOR_SIDE, w_mix, on_vector, 0, 1)
+        for a, j in ((1, 1), (0, 2), (1, 2)):
+            at(-1, SCALAR_MIX, w_mix, on_scalar, a, j)
+        for j in range(1, J):
+            for a in range(A):
                 at(PACK * j - AHEAD - 1 + a, VECTOR_SIDE, w_quantise, a, j)
+        for t in range(2, PACK):
+            at(-1, VECTOR_SIDE, x_turned_quantise, 0, t)
         for t in range(PACK):
-            at(X_TURN[t // 2], TURN, x_turn, 1, t)
+            at(X_TURN, TURN, x_turn, 1, t)
             at(HALF + t - AHEAD - 2, VECTOR_SIDE, x_turned_quantise, 1, t)
 
         for pair in range(2):
-            last_weighed = HALF - 2 + 2 * pair
+            complete = HALF - 2 + 2 * pair
             for j in range(J):
-                at(min(PACK * j + PACK, last_weighed) + 1, TURN, h_turn, 0, j, pair)
-                at(last_weighed + 3, VECTOR_SIDE, h_turned_quantise, 0, j, pair)
-                at(HALF + last_weighed + 1, TURN, h_turn, 1, j, pair)
-                at(TILES + 2 + pair, VECTOR_SIDE, h_turned_quantise, 1, j, pair)
+                at((PACK, HALF - 2, complete)[j], TURN, h_turn, on_scalar, 0, j, pair)
+                at(complete + 2, VECTOR_SIDE, h_turned_quantise, 0, j, pair)
             for n in range(2 * A):
-                at(last_weighed + 3 + n, PRODUCT, dx_product, on_scalar, 0, 2 * pair + n // A, n % A)
+                at(complete + 2 + n, PRODUCT, dx_product, on_scalar, 0, 2 * pair + n // A, n % A)
+        last_turn = DW_START + K // P
+        for j in range(J):
+            for pair in range(2):
+                at(last_turn, TURN, h_turn, (on_vector, on_scalar)[pair], 1, j, pair)
+        for pair in range(2):
+            for j in range(J):
+                at(last_turn + 2, VECTOR_SIDE, h_turned_quantise, 1, j, pair)
 
         for a in range(A):
             at(HALF + 2 * a, SCALAR_MIX, x_mix, on_scalar, 1, a)
-            at(DW_START - 2 + 2 * a, VECTOR_SIDE, x_mixed_quantise, 1, a)
+            for g in range(G):
+                at(DW_START - 3 + 2 * a + g, VECTOR_SIDE, x_mixed_quantise, g, a)
         at(H_MIX, SCALAR_MIX, h_mix, on_scalar, 0, 0)
         at(HALF + PACK, SCALAR_MIX, h_mix, on_scalar, 0, 1)
         at(TILES, VECTOR_SIDE, h_mix, on_vector, 0, 2)
@@ -257,7 +262,7 @@ def tile_binary_hinge_backward_s8_kernel(tc, x, wb, c, r, v_words, v_scales, out
         products = products + [(dx_product, 1, t, a) for t in range(PACK) for a in range(A)]
         for n, (job, *args) in enumerate(products):
             step = DW_START + n // 2
-            at(step, PRODUCT, job, on_vector if step > TILES + 3 and n % 2 == 0 else on_scalar, *args)
+            at(step, PRODUCT, job, on_vector if step >= last_turn + 2 and n % 2 == 0 else on_scalar, *args)
 
         for key in sorted(due):
             for job, args in due[key]:

@@ -26,8 +26,8 @@ HALF = J * PACK
 SUBTRACT, SCALAR_MIX, WEIGH, VECTOR_SIDE, MARGINS, TURN, PRODUCT = range(7)
 
 AHEAD = 2
-X_TURN = 5
-H_MIX = 8
+X_TURN = (5, 8)
+H_MIX = 7
 DW_START = 18
 
 
@@ -69,14 +69,14 @@ def tile_binary_hinge_backward_s8_kernel(tc, x, wb, c, r, v_words, v_scales, out
                 c_sb[g, j] = tile[:, :, (j - j0) * PASS : (j - j0 + 1) * PASS]
 
         load_x(0, 0, 2)
-        load_w(0, 0)
         load_x(0, 2, 4)
-        load_w(1, 0)
-        load_c(0, 0, 1)
-        nc.sync.dma_start(out=r_sb[:], in_=r.rearrange("(g p t) -> p g t", p=P, t=PACK))
-        for j in range(1, J):
+        for j in range(2):
             for a in range(A):
                 load_w(a, j)
+        load_c(0, 0, 1)
+        nc.sync.dma_start(out=r_sb[:], in_=r.rearrange("(g p t) -> p g t", p=P, t=PACK))
+        for a in range(A):
+            load_w(a, 2)
         load_c(0, 1, 2)
         load_x(1, 0, 4)
         load_c(0, 2, 3)
@@ -189,23 +189,27 @@ def tile_binary_hinge_backward_s8_kernel(tc, x, wb, c, r, v_words, v_scales, out
 
         def dw_product(copy, kt, j):
             multiply("dw", [columns(x_by_m[g, kt // PACK], kt % PACK * P, P) + columns(h_by_m[g, j], 0, PASS) for g in range(G)])
-            block = work.tile([P, PASS], F32, name="dw_block", tag="dw_block", bufs=8)
+            block = work.tile([P, PASS], F32, name="dw_block", tag="dw_block", bufs=9)
             copy(out=block[:].rearrange("p (q u e) -> p q u e", u=2, e=2),
                  in_=live["dw"][:].rearrange("p (u q e) -> p q u e", u=2, e=2))
             nc.sync.dma_start(out=out_1[kt * P : (kt + 1) * P, j * PASS : (j + 1) * PASS], in_=block[:])
 
+        x_mix(on_vector, 0, 1)
+        x_turn(0, 0)
         w_mix(on_vector, 0, 0)
-        for t in range(2):
-            x_turn(0, t)
-        w_quantise(0, 0)
-        for t in range(2):
-            x_turned_quantise(0, t)
         x_mix(on_scalar, 0, 0)
-        for t in range(2, PACK):
+        for t in range(1, PACK):
             x_turn(0, t)
+        x_turned_quantise(0, 0)
         w_mix(on_vector, 1, 0)
-        w_quantise(1, 0)
-        x_mix(on_scalar, 0, 1)
+        for a in range(A):
+            w_quantise(a, 0)
+        w_mix(on_vector, 0, 1)
+        for t in range(1, PACK):
+            x_turned_quantise(0, t)
+        w_quantise(0, 1)
+        for a, j in ((1, 1), (0, 2), (1, 2)):
+            w_mix(on_scalar, a, j)
 
         due = {}
 
@@ -218,17 +222,12 @@ def tile_binary_hinge_backward_s8_kernel(tc, x, wb, c, r, v_words, v_scales, out
             at(i, SUBTRACT, subtract, *tile_i)
             at(i + 1, WEIGH, weigh, *tile_i)
 
-        at(0, VECTOR_SIDE, w_mix, on_vector, 0, 1)
-        for a, j in ((1, 1), (0, 2), (1, 2)):
-            at(-1, SCALAR_MIX, w_mix, on_scalar, a, j)
-        for j in range(1, J):
-            for a in range(A):
-                at(PACK * j - AHEAD - 1 + a, VECTOR_SIDE, w_quantise, a, j)
-        for t in range(2, PACK):
-            at(-1, VECTOR_SIDE, x_turned_quantise, 0, t)
+        at(0, VECTOR_SIDE, w_quantise, 1, 1)
+        for a in range(A):
+            at(2 * PACK - AHEAD - 2 + a, VECTOR_SIDE, w_quantise, a, 2)
         for t in range(PACK):
-            at(X_TURN, TURN, x_turn, 1, t)
-            at(HALF + t - AHEAD - 2, VECTOR_SIDE, x_turned_quantise, 1, t)
+            at(X_TURN[t // 2], TURN, x_turn, 1, t)
+            at(HALF + t - AHEAD - 1, VECTOR_SIDE, x_turned_quantise, 1, t)
 
         for pair in range(2):
             complete = HALF - 2 + 2 * pair
@@ -236,7 +235,7 @@ def tile_binary_hinge_backward_s8_kernel(tc, x, wb, c, r, v_words, v_scales, out
                 at((PACK, HALF - 2, complete)[j], TURN, h_turn, on_scalar, 0, j, pair)
                 at(complete + 2, VECTOR_SIDE, h_turned_quantise, 0, j, pair)
             for n in range(2 * A):
-                at(complete + 2 + n, PRODUCT, dx_product, on_scalar, 0, 2 * pair + n // A, n % A)
+                at(complete + 3 + n, PRODUCT, dx_product, on_scalar, 0, 2 * pair + n // A, n % A)
         last_turn = DW_START + K // P
         for j in range(J):
             for pair in range(2):
@@ -246,11 +245,11 @@ def tile_binary_hinge_backward_s8_kernel(tc, x, wb, c, r, v_words, v_scales, out
                 at(last_turn + 2, VECTOR_SIDE, h_turned_quantise, 1, j, pair)
 
         for a in range(A):
-            at(HALF + 2 * a, SCALAR_MIX, x_mix, on_scalar, 1, a)
+            at(DW_START - 4 + 2 * a, SCALAR_MIX, x_mix, on_scalar, 1, a)
             for g in range(G):
                 at(DW_START - 3 + 2 * a + g, VECTOR_SIDE, x_mixed_quantise, g, a)
         at(H_MIX, SCALAR_MIX, h_mix, on_scalar, 0, 0)
-        at(HALF + PACK, SCALAR_MIX, h_mix, on_scalar, 0, 1)
+        at(DW_START, SCALAR_MIX, h_mix, on_scalar, 0, 1)
         at(TILES, VECTOR_SIDE, h_mix, on_vector, 0, 2)
         for j in range(J):
             weighed = HALF + PACK * j + PACK

from contextlib import ExitStack

import concourse.mybir as mybir
from concourse.masks import make_identity

M, K, N = 1024, 1024, 1536
FLOPS = 3 * 2 * M * K * N

F32 = mybir.dt.float32
BF16 = mybir.dt.bfloat16
U32 = mybir.dt.uint32
I32 = mybir.dt.int32
U8 = mybir.dt.uint8
FP8X4 = mybir.dt.float8_e4m3fn_x4
FP4X4 = mybir.dt.float4_e2m1fn_x4
ALU = mybir.AluOpType

P = 128
PACK = 4
PASS = P * PACK
G, A, J = M // PASS, K // PASS, N // PASS
RUN = 4
TILES = G * J * PACK
HALF = J * PACK

SUBTRACT, SCALAR_MIX, WEIGH, VECTOR_SIDE, MARGINS, TURN, PRODUCT = range(7)

AHEAD = 2
X_TURN = (5, 8)
H_MIX = 7
DW_START = 18


def tile_binary_hinge_backward_s8_kernel(tc, x, wb, c, r, v_words, v_scales, out_0, out_1):
    nc = tc.nc
    on_vector, on_scalar = nc.vector.tensor_copy, nc.scalar.copy
    with ExitStack() as ctx:
        keep = ctx.enter_context(tc.tile_pool(name="keep", bufs=1))
        work = ctx.enter_context(tc.tile_pool(name="work", bufs=3))
        psum = ctx.enter_context(tc.psum_pool(name="psum", bufs=8))
        ctx.enter_context(tc.manual_schedule())

        ident = keep.tile([P, P], F32, name="ident")
        make_identity(nc, ident[:])
        v_plane = keep.tile([P, J * K], U8, name="v_plane", align_bytes=64)
        nc.vector.memset(v_plane[:].bitcast(I32), 0)

        x_rows = x.rearrange("(g p t) k -> g p t k", p=P, t=PACK)
        c_rows = c.rearrange("(g p t) n -> g p t n", p=P, t=PACK)
        w_rows = wb.rearrange("(a p t) n -> a p t n", p=P, t=PACK)
        dx_rows = out_0.rearrange("(g p t) k -> g p t k", p=P, t=PACK)

        x_sb = [keep.tile([P, PACK * K], BF16, name="x_sb%d" % g) for g in range(G)]
        r_sb = keep.tile([P, G, PACK], BF16, name="r_sb")
        v_sb = keep.tile([P, J, 2 * K], U8, name="v_sb", align_bytes=64)
        w_sb, c_sb = {}, {}

        def load_x(g, t0, t1):
            nc.sync.dma_start(out=x_sb[g][:, t0 * K : t1 * K].rearrange("p (t k) -> p t k", k=K), in_=x_rows[g][:, t0:t1, :])

        def load_w(a, j):
            w_sb[a, j] = work.tile([P, PACK, PASS], BF16, name="w_sb", tag="row", bufs=A * J)
            nc.sync.dma_start(out=w_sb[a, j][:], in_=w_rows[a][:, :, j * PASS : (j + 1) * PASS])

        def load_c(g, j0, j1):
            tile = keep.tile([P, PACK, (j1 - j0) * PASS], BF16, name="c_sb%d%d" % (g, j0))
            nc.sync.dma_start(out=tile[:], in_=c_rows[g][:, :, j0 * PASS : j1 * PASS])
            for j in range(j0, j1):
                c_sb[g, j] = tile[:, :, (j - j0) * PASS : (j - j0 + 1) * PASS]

        load_x(0, 0, 2)
        load_x(0, 2, 4)
        for j in range(2):
            for a in range(A):
                load_w(a, j)
        load_c(0, 0, 1)
        nc.sync.dma_start(out=r_sb[:], in_=r.rearrange("(g p t) -> p g t", p=P, t=PACK))
        for a in range(A):
            load_w(a, 2)
        load_c(0, 1, 2)
        load_x(1, 0, 4)
        load_c(0, 2, 3)
        load_c(1, 0, 1)
        nc.sync.dma_start(out=v_sb[:].bitcast(I32), in_=v_words.rearrange("j p b -> p j b").bitcast(I32))
        for q in range(4):
            nc.sync.dma_start(
                out=v_plane[32 * q : 32 * q + 4, :].rearrange("s (j k) -> s j k", j=J).bitcast(I32),
                in_=v_scales[:, 4 * q : 4 * q + 4, :].rearrange("j s k -> s j k").bitcast(I32),
            )
        load_c(1, 1, 3)

        def quantised(name, width):
            codes = keep.tile([P, width], U32, name=name + "_codes", align_bytes=64)
            scales = keep.tile([P, width], U8, name=name + "_scales", align_bytes=64)
            return codes, scales

        x_by_k = {(g, t): quantised("xk%d%d" % (g, t), A * P) for g in range(G) for t in range(PACK)}
        x_by_m = {(g, a): quantised("xm%d%d" % (g, a), PASS) for g in range(G) for a in range(A)}
        w_by_k = {(a, j): quantised("wq%d%d" % (a, j), PASS) for a in range(A) for j in range(J)}
        h_by_m = {(g, j): quantised("hm%d%d" % (g, j), PASS) for g in range(G) for j in range(J)}
        h_by_n = {(g, j, pair): quantised("hn%d%d%d" % (g, j, pair), 2 * P) for g in range(G) for j in range(J) for pair in range(2)}
        live = {}

        def quantise(operand, key):
            nc.vector.quantize_mx(out=operand[0][:].bitcast(FP8X4), scales=operand[1][:], in_=live[key][:])

        def multiply(key, passes):
            live[key] = psum.tile([P, PASS], F32, name="bank", tag="bank")
            for n, (lhsT, lhsT_scale, rhs, rhs_scale) in enumerate(passes):
                nc.tensor.matmul_mx(out=live[key][:], lhsT=lhsT, lhsT_scale=lhsT_scale, rhs=rhs, rhs_scale=rhs_scale,
                                    start=(n == 0), stop=(n == len(passes) - 1))

        def columns(operand, first, width):
            return operand[0][:, first : first + width].bitcast(FP8X4), operand[1][:, first : first + width]

        def mix(copy, key, rows, tag, bufs):
            live[key] = work.tile([P, PACK * PASS], BF16, name=tag, tag=tag, bufs=bufs, align_bytes=64)
            copy(out=live[key][:].rearrange("p (c i t) -> p c t i", i=RUN, t=PACK), in_=rows.rearrange("p t (c i) -> p c t i", i=RUN))

        def turn(copy, key, blocks):
            bank = psum.tile([P, PASS], F32, name="bank", tag="bank")
            for n, block in enumerate(blocks):
                nc.tensor.transpose(bank[:, n * P : (n + 1) * P], block, ident[:])
            live[key] = work.tile([P, 2 * PASS], BF16, name="turned", tag="turned", bufs=9, align_bytes=64)
            copy(out=live[key][:].bitcast(F32).rearrange("p (b m u) -> p b m u", b=2, u=2),
                 in_=bank[:].rearrange("p (b u m) -> p b m u", b=2, u=2))

        def x_turn(g, t):
            words = x_sb[g][:, t * K : (t + 1) * K].bitcast(F32)
            turn(on_scalar, ("x turned", g, t), [words[:, 2 * P * a + u : 2 * P * (a + 1) : 2] for a in range(A) for u in range(2)])

        def x_turned_quantise(g, t):
            quantise(x_by_k[g, t], ("x turned", g, t))

        def x_mix(copy, g, a):
            rows = x_sb[g][:].rearrange("p (t k) -> p t k", t=PACK)[:, :, a * PASS : (a + 1) * PASS]
            mix(copy, ("x mixed", g, a), rows, "x_mixed", G * A)

        def x_mixed_quantise(g, a):
            quantise(x_by_m[g, a], ("x mixed", g, a))

        def w_mix(copy, a, j):
            mix(copy, ("w mixed", a, j), w_sb[a, j][:], "mixed", 4)

        def w_quantise(a, j):
            quantise(w_by_k[a, j], ("w mixed", a, j))

        def margins(g, j, t):
            multiply(("z", g, j, t), [columns(x_by_k[g, t], a * P, P) + columns(w_by_k[a, j], 0, PASS) for a in range(A)])

        def subtract(g, j, t):
            live["d", g, j, t] = work.tile([P, PASS], F32, name="d", tag="d")
            nc.vector.tensor_tensor(out=live["d", g, j, t][:].rearrange("p (u q e) -> p u q e", u=2, e=2),
                                    in0=c_sb[g, j][:, t, :].rearrange("p (q u e) -> p u q e", u=2, e=2),
                                    in1=live["z", g, j, t][:].rearrange("p (q u e) -> p u q e", u=2, e=2),
                                    op=ALU.subtract)

        def weigh(g, j, t):
            if t == 0:
                live["h", g, j] = work.tile([P, PACK * PASS], BF16, name="h", tag="h", bufs=G * J)
            nc.vector.tensor_scalar(out=live["h", g, j][:, t * PASS : (t + 1) * PASS], in0=live["d", g, j, t][:],
                                    scalar1=0.0, scalar2=r_sb[:, g, t : t + 1], op0=ALU.max, op1=ALU.mult)

        def h_turn(copy, g, j, pair):
            words = live["h", g, j][:].bitcast(F32)
            turn(copy, ("h turned", g, j, pair), [words[:, (4 * pair + n) * P : (4 * pair + n + 1) * P] for n in range(4)])

        def h_turned_quantise(g, j, pair):
            quantise(h_by_n[g, j, pair], ("h turned", g, j, pair))

        def h_mix(copy, g, j):
            mix(copy, ("h mixed", g, j), live["h", g, j][:].rearrange("p (t n) -> p t n", t=PACK), "mixed", 4)

        def h_mixed_quantise(g, j):
            quantise(h_by_m[g, j], ("h mixed", g, j))

        def dx_product(copy, g, t, a):
            multiply("dx", [columns(h_by_n[g, j, t // 2], t % 2 * P, P)
                            + (v_sb[:, j, 2 * a * PASS : 2 * (a + 1) * PASS].bitcast(FP4X4),
                               v_plane[:, j * K + a * PASS : j * K + (a + 1) * PASS]) for j in range(J)])
            if a == 0:
                live["dx row", g, t] = work.tile([P, K], F32, name="dx_row", tag="row", bufs=A * J)
            row, cols = live["dx row", g, t], slice(a * PASS, (a + 1) * PASS)
            copy(out=row[:, cols], in_=live["dx"][:])
            if (g, t // 2) == (G - 1, 1):
                nc.sync.dma_start(out=dx_rows[g][:, t, cols], in_=row[:, cols])
            elif a == A - 1:
                nc.sync.dma_start(out=dx_rows[g][:, t, :], in_=row[:])

        def dw_product(copy, kt, j):
            multiply("dw", [columns(x_by_m[g, kt // PACK], kt % PACK * P, P) + columns(h_by_m[g, j], 0, PASS) for g in range(G)])
            block = work.tile([P, PASS], F32, name="dw_block", tag="dw_block", bufs=9)
            copy(out=block[:].rearrange("p (q u e) -> p q u e", u=2, e=2),
                 in_=live["dw"][:].rearrange("p (u q e) -> p q u e", u=2, e=2))
            nc.sync.dma_start(out=out_1[kt * P : (kt + 1) * P, j * PASS : (j + 1) * PASS], in_=block[:])

        x_mix(on_vector, 0, 1)
        x_turn(0, 0)
        w_mix(on_vector, 0, 0)
        x_mix(on_scalar, 0, 0)
        for t in range(1, PACK):
            x_turn(0, t)
        x_turned_quantise(0, 0)
        w_mix(on_vector, 1, 0)
        for a in range(A):
            w_quantise(a, 0)
        w_mix(on_vector, 0, 1)
        for t in range(1, PACK):
            x_turned_quantise(0, t)
        w_quantise(0, 1)
        for a, j in ((1, 1), (0, 2), (1, 2)):
            w_mix(on_scalar, a, j)

        due = {}

        def at(step, phase, job, *args):
            due.setdefault((step, phase), []).append((job, args))

        tiles = [(g, j, t) for g in range(G) for j in range(J) for t in range(PACK)]
        for i, tile_i in enumerate(tiles):
            at(i - AHEAD, MARGINS, margins, *tile_i)
            at(i, SUBTRACT, subtract, *tile_i)
            at(i + 1, WEIGH, weigh, *tile_i)

        at(0, VECTOR_SIDE, w_quantise, 1, 1)
        for a in range(A):
            at(2 * PACK - AHEAD - 2 + a, VECTOR_SIDE, w_quantise, a, 2)
        for t in range(PACK):
            at(X_TURN[t // 2], TURN, x_turn, 1, t)
            at(HALF + t - AHEAD - 1, VECTOR_SIDE, x_turned_quantise, 1, t)

        for pair in range(2):
            complete = HALF - 2 + 2 * pair
            for j in range(J):
                at((PACK, HALF - 2, complete)[j], TURN, h_turn, on_scalar, 0, j, pair)
                at(complete + 2, VECTOR_SIDE, h_turned_quantise, 0, j, pair)
            for n in range(2 * A):
                at(complete + 3 + n, PRODUCT, dx_product, on_scalar, 0, 2 * pair + n // A, n % A)
        last_turn = DW_START + K // P
        for j in range(J):
            for pair in range(2):
                at(last_turn, TURN, h_turn, (on_vector, on_scalar)[pair], 1, j, pair)
        for pair in range(2):
            for j in range(J):
                at(last_turn + 2, VECTOR_SIDE, h_turned_quantise, 1, j, pair)

        for a in range(A):
            at(DW_START - 4 + 2 * a, SCALAR_MIX, x_mix, on_scalar, 1, a)
            for g in range(G):
                at(DW_START - 3 + 2 * a + g, VECTOR_SIDE, x_mixed_quantise, g, a)
        at(H_MIX, SCALAR_MIX, h_mix, on_scalar, 0, 0)
        at(DW_START, SCALAR_MIX, h_mix, on_scalar, 0, 1)
        at(TILES, VECTOR_SIDE, h_mix, on_vector, 0, 2)
        for j in range(J):
            weighed = HALF + PACK * j + PACK
            at(weighed, VECTOR_SIDE, h_mix, on_vector, 1, j)
            for g in range(G):
                at(weighed + 1, VECTOR_SIDE, h_mixed_quantise, g, j)

        products = [(dw_product, kt, j) for j in range(J) for kt in range(K // P)]
        products = products + [(dx_product, 1, t, a) for t in range(PACK) for a in range(A)]
        for n, (job, *args) in enumerate(products):
            step = DW_START + n // 2
            at(step, PRODUCT, job, on_vector if step >= last_turn + 2 and n % 2 == 0 else on_scalar, *args)

        for key in sorted(due):
            for job, args in due[key]:
                job(*args)
